import numpy as np, ml_dtypes
CORES = [83,85,87,115,117,119]
N = 6
import mx_ref
NC, G = 256, 4
C = np.float32(0.047)
BF = ml_dtypes.bfloat16
def cut(t, i, w=512):
    return t[:, w * i:w * i + w]
def tile(rs):
    return np.stack(rs, axis=2).reshape(128, -1).astype(BF)
def layer(w, X):
    out = []
    for i in range(G):
        for t in range(len(X)):
            p = mx_ref.matmul(mx_ref.quantize(cut(w, len(X) * i + t)), X[t])
            z = p if t == 0 else z + p
        out.append(z)
    return out
def setup_inputs(rng):
    def f(*shape):
        return mx_ref.flush((rng.standard_normal(shape, dtype=np.float32) * np.exp2(rng.integers(-2, 3, shape[:-1] + (1,)))).astype(BF))
    return {"x": f(N, 128, 4 * NC), "w": f(N, 128, 512), "a": np.broadcast_to(f(1, 128, 4 * 512), (N, 128, 4 * 512)).copy(), "bb": f(N, 128, 512)}
def setup_inputs_blocks(rng):
    d = setup_inputs(rng)
    for k in ("x", "w", "bb"): d[k] = mx_ref.spread(d[k], rng, 4)
    return d
def setup_inputs_wide(rng):
    d = setup_inputs(rng)
    for k in ("x", "w", "bb"): d[k] = mx_ref.flush((d[k].astype(np.float32) * np.exp2(rng.integers(-6, 7, (N, 1, 1))).astype(np.float32)).astype(BF))
    return d
def setup_inputs_zeros(rng):
    d = setup_inputs(rng); v = d["x"].reshape(N, 128, -1, 4).copy()
    v[np.broadcast_to((rng.random((N, 1, v.shape[2], 1)) < 0.33), v.shape)] = 0
    d["x"] = v.reshape(d["x"].shape)
    return d
def reference(x, w, a, bb):
    X = [mx_ref.quantize(x[j]) for j in range(N)]
    T = [mx_ref.quantize(tile([z * C for z in layer(a[j], [X[j]])])) for j in range(N)]
    y = np.zeros((N, 128, N * NC), np.float32)
    for r in range(N):
        qw = mx_ref.quantize(w[r]); qb = mx_ref.quantize(bb[r])
        for j in range(N):
            y[r][:, NC * j:NC * j + NC] = mx_ref.matmul(qw, X[j]) + mx_ref.matmul(qb, T[j])
    return {"y": y}

@@ -1,0 +1,178 @@
+import numpy as np
+from concourse.bass import DstId, RemoteDMATransfer
+from concourse.mybir import dt, AluOpType, ActivationFunctionType
+
+N, NC, G = 6, 256, 4
+SW = 128
+FACTOR = float(np.float32(0.047))
+
+SCRATCH = {
+    "xin": ("sbuf", [128, 4 * NC], "bfloat16"),
+    "ain": ("sbuf", [128, 4 * SW * G], "bfloat16"),
+    "win": ("sbuf", [128, 4 * SW], "bfloat16"),
+    "bin": ("sbuf", [128, 4 * SW], "bfloat16"),
+    "ac": ("sbuf", [128, SW * G], "float8_e4m3fn_x4"),
+    "asc": ("sbuf", [128, SW * G], "uint8"),
+    "wc": ("sbuf", [128, SW], "float8_e4m3fn_x4"),
+    "wsc": ("sbuf", [128, SW], "uint8"),
+    "bc": ("sbuf", [128, SW], "float8_e4m3fn_x4"),
+    "bsc": ("sbuf", [128, SW], "uint8"),
+    "qc": ("sbuf", [128, 2 * NC * N], "float8_e4m3fn_x4"),
+    "qs": ("sbuf", [128, 2 * NC * N], "uint8"),
+    "yo": ("sbuf", [128, N * NC], "float32"),
+    "ps": ("psum", [128, 512 * 8], "float32"),
+}
+SEMAPHORES = ["lx", "la0", "la1", "lw", "lb", "qx", "qa0", "qa1", "qw", "qb", "sent", "st"]
+for _j in range(N):
+    SCRATCH["tb%d" % _j] = ("sbuf", [128, 4 * NC], "bfloat16")
+    SEMAPHORES += ["%s%d" % (k, _j) for k in ("ax", "at", "tq", "yd", "ev")]
+    SEMAPHORES += ["%s%d_%d" % (k, _j, b) for k in ("mt", "sc") for b in range(G)]
+
+
+def ones(mask):
+    return bin(mask).count("1")
+
+
+def rank_program(g, core, T, topo):
+    r = T.rank_of(core)
+    if r is None:
+        return
+    S, cores = T.sem, T.cores
+    ten, vec, act, sync = g.tensor, g.vector, g.scalar, g.sync
+
+    mine = [j for j in range(N) if topo.chip(cores[j]) == topo.chip(core)]
+    far = [j for j in range(N) if j not in mine]
+    k = len(mine)
+    pos = mine.index(r)
+    nxt, prv = mine[(pos + 1) % k], mine[(pos - 1) % k]
+    p = far[pos]
+    fa = far[(pos - 1) % k]
+    fb = far[(pos + 1) % k]
+    OFF = topo.mask(core, cores[p])
+    ON = topo.mask(core, cores[nxt])
+
+    def die_mates(j):
+        return sum(topo.chip(cores[i]) == topo.chip(cores[j]) and topo.die(cores[i]) == topo.die(cores[j]) for i in range(N))
+
+    def xcols(j):
+        return slice(2 * NC * j, 2 * NC * j + NC)
+
+    def tcols(j):
+        return slice(2 * NC * j + NC, 2 * NC * j + 2 * NC)
+
+    def both(j):
+        return slice(2 * NC * j, 2 * NC * j + 2 * NC)
+
+    sync.dma_start(T.xin[:], T.x[:]).then_inc(S["lx"], 16)
+    half = 2 * SW * G
+    for h in (0, 1):
+        sync.dma_start(T.ain[:, h * half:(h + 1) * half], T.a[:, h * half:(h + 1) * half]).then_inc(S["la%d" % h], 16)
+    sync.dma_start(T.win[:], T.w[:]).then_inc(S["lw"], 16)
+    sync.dma_start(T.bin[:], T.bb[:]).then_inc(S["lb"], 16)
+
+    out = []
+
+    def send(cols, dsts, mask, sem):
+        ids = []
+        for d in dsts:
+            rid, pid = topo.addr(cores[d])[:2]
+            ids.append(DstId(rid=rid, pnc=pid))
+        for view in (T.qc[:, cols].bitcast(dt.uint8), T.qs[:, cols]):
+            g.remote_dma_fused([RemoteDMATransfer(dst_ids=ids, dma_engine_mask=mask, remote_sem=S[sem],
+                                                  srcs=[view], dsts=[view] * len(ids))], local_sem=S["sent"])
+            out.append(ones(mask))
+
+    g.wait_ge(S["qx"], 1)
+    send(xcols(r), [p], OFF, "ax%d" % r)
+    g.wait_ge(S["tq%d" % r], 1)
+    send(both(r), [nxt, prv], ON, "at%d" % r)
+    g.wait_ge(S["ax%d" % p], 2 * ones(OFF))
+    send(xcols(p), [nxt, prv], ON, "ax%d" % p)
+    g.wait_ge(S["tq%d" % p], 1)
+    send(tcols(p), [prv], ON, "at%d" % p)
+    g.wait_ge(S["sent"], sum(out))
+
+    x_here = {r: ("qx", 1), p: ("ax%d" % p, 2 * ones(OFF))}
+    t_here = {j: ("tq%d" % j, 1) for j in (r, p, fa)}
+    for j in (nxt, prv):
+        x_here[j] = t_here[j] = ("at%d" % j, 2 * ones(ON))
+    for j in (fa, fb):
+        x_here[j] = ("ax%d" % j, 2 * ones(ON))
+    t_here[fb] = ("at%d" % fb, 2 * ones(ON))
+
+    seq = [("t", r), ("w", r), ("b", r), ("t", p), ("w", nxt), ("w", prv), ("b", nxt), ("b", prv), ("w", p), ("b", p)]
+    if die_mates(fb) < die_mates(fa):
+        seq += [("t", fa), ("w", fb), ("b", fb), ("w", fa), ("b", fa)]
+    else:
+        seq += [("t", fa), ("w", fa), ("w", fb), ("b", fa), ("b", fb)]
+    order = [j for kind, j in seq if kind == "b"]
+    ybank, before = {}, {}
+    opened = [j for kind, j in seq if kind == "w"]
+    for i, j in enumerate(opened):
+        ybank[j] = G + i % (8 - G)
+        before[j] = opened[i - (8 - G)] if i >= 8 - G else None
+
+    def bank(i):
+        return T.ps[:, 512 * i:512 * i + NC]
+
+    vec.wait_ge(S["lx"], 16)
+    vec.quantize_mx(T.qc[:, xcols(r)], T.qs[:, xcols(r)], T.xin[:]).then_inc(S["qx"], 1)
+    for h in (0, 1):
+        c = slice(2 * SW * h, 2 * SW * h + 2 * SW)
+        vec.wait_ge(S["la%d" % h], 16)
+        vec.quantize_mx(T.ac[:, c], T.asc[:, c], T.ain[:, h * half:(h + 1) * half]).then_inc(S["qa%d" % h], 1)
+
+    last_t = None
+    for kind, j in seq:
+        X = (T.qc[:, xcols(j)], T.qs[:, xcols(j)])
+        tt = (T.qc[:, tcols(j)], T.qs[:, tcols(j)])
+        if kind == "t":
+            ten.wait_ge(S[x_here[j][0]], x_here[j][1])
+            for b in range(G):
+                if last_t is None:
+                    ten.wait_ge(S["qa%d" % (b // 2)], 1)
+                else:
+                    ten.wait_ge(S["sc%d_%d" % (last_t, b)], 1)
+                c = slice(SW * b, SW * b + SW)
+                ten.matmul_mx(bank(b), T.ac[:, c], T.asc[:, c], X[0], X[1], True, True).then_inc(S["mt%d_%d" % (j, b)], 1)
+                cols = T["tb%d" % j][:, b:G * NC:G]
+                if b % 2 == 0:
+                    act.wait_ge(S["mt%d_%d" % (j, b)], 1)
+                    act.activation(cols, bank(b), ActivationFunctionType.Copy, scale=FACTOR).then_inc(S["sc%d_%d" % (j, b)], 1)
+                else:
+                    vec.wait_ge(S["mt%d_%d" % (j, b)], 1)
+                    vec.tensor_scalar(cols, bank(b), FACTOR, None, AluOpType.mult).then_inc(S["sc%d_%d" % (j, b)], 1)
+            for b in range(G):
+                vec.wait_ge(S["sc%d_%d" % (j, b)], 1)
+            vec.quantize_mx(tt[0], tt[1], T["tb%d" % j][:]).then_inc(S["tq%d" % j], 1)
+            if last_t is None:
+                vec.wait_ge(S["lw"], 16)
+                vec.quantize_mx(T.wc[:], T.wsc[:], T.win[:]).then_inc(S["qw"], 1)
+                vec.wait_ge(S["lb"], 16)
+                vec.quantize_mx(T.bc[:], T.bsc[:], T.bin[:]).then_inc(S["qb"], 1)
+            last_t = j
+        elif kind == "w":
+            ten.wait_ge(S["qw"], 1)
+            ten.wait_ge(S[x_here[j][0]], x_here[j][1])
+            if before[j] is not None:
+                ten.wait_ge(S["ev%d" % before[j]], 1)
+            ten.matmul_mx(bank(ybank[j]), T.wc[:], T.wsc[:], X[0], X[1], True, False)
+        else:
+            ten.wait_ge(S["qb"], 1)
+            ten.wait_ge(S[t_here[j][0]], t_here[j][1])
+            ten.matmul_mx(bank(ybank[j]), T.bc[:], T.bsc[:], tt[0], tt[1], False, True).then_inc(S["yd%d" % j], 1)
+            dst = T.yo[:, NC * j:NC * j + NC]
+            q = act if order.index(j) % 2 == 0 else vec
+            q.wait_ge(S["yd%d" % j], 1)
+            if q is act:
+                act.activation(dst, bank(ybank[j]), ActivationFunctionType.Copy).then_inc(S["ev%d" % j], 1)
+            else:
+                vec.tensor_copy(dst, bank(ybank[j])).then_inc(S["ev%d" % j], 1)
+
+    groups = [mine] + [[j] for j in order if j in far]
+    for js in groups:
+        for j in js:
+            sync.wait_ge(S["ev%d" % j], 1)
+        c = slice(NC * js[0], NC * js[-1] + NC)
+        sync.dma_start(T.y[:, c], T.yo[:, c]).then_inc(S["st"], 16)
+    sync.wait_ge(S["st"], 16 * len(groups))

@@ -3,14 +3,18 @@ from concourse.bass import DstId, RemoteDMATransfer
 from concourse.mybir import dt, AluOpType, ActivationFunctionType
 
 N, NC, G = 6, 256, 4
+HC = NC // 2
 SW = 128
 FACTOR = float(np.float32(0.047))
+HALVES = (0, 1)
 
 SCRATCH = {
     "xin": ("sbuf", [128, 4 * NC], "bfloat16"),
     "ain": ("sbuf", [128, 4 * SW * G], "bfloat16"),
     "win": ("sbuf", [128, 4 * SW], "bfloat16"),
     "bin": ("sbuf", [128, 4 * SW], "bfloat16"),
+    "t0": ("sbuf", [128, 4 * NC], "bfloat16"),
+    "t1": ("sbuf", [128, 4 * NC], "bfloat16"),
     "ac": ("sbuf", [128, SW * G], "float8_e4m3fn_x4"),
     "asc": ("sbuf", [128, SW * G], "uint8"),
     "wc": ("sbuf", [128, SW], "float8_e4m3fn_x4"),
@@ -22,11 +26,13 @@ SCRATCH = {
     "yo": ("sbuf", [128, N * NC], "float32"),
     "ps": ("psum", [128, 512 * 8], "float32"),
 }
-SEMAPHORES = ["lx", "la0", "la1", "lw", "lb", "qx", "qa0", "qa1", "qw", "qb", "sent", "st"]
+SEMAPHORES = ["lx0", "lx1", "la0", "la1", "lw", "lb", "qx0", "qx1", "qa0", "qa1", "qw", "qb", "sent", "st"]
 for _j in range(N):
-    SCRATCH["tb%d" % _j] = ("sbuf", [128, 4 * NC], "bfloat16")
-    SEMAPHORES += ["%s%d" % (k, _j) for k in ("ax", "at", "tq", "yd", "ev")]
-    SEMAPHORES += ["%s%d_%d" % (k, _j, b) for k in ("mt", "sc") for b in range(G)]
+    SEMAPHORES += ["%s%d" % (s, _j) for s in ("ah", "ax", "at")]
+    SEMAPHORES += ["%s%d_%d" % (s, _j, h) for s in ("yd", "ev") for h in HALVES]
+for _u in (0, 1):
+    SEMAPHORES += ["tq%d_%d" % (_u, h) for h in HALVES]
+    SEMAPHORES += ["%s%d_%d_%d" % (s, _u, h, b) for s in ("mt", "sc") for h in HALVES for b in range(G)]
 
 
 def ones(mask):
@@ -45,134 +51,162 @@ def rank_program(g, core, T, topo):
     k = len(mine)
     pos = mine.index(r)
     nxt, prv = mine[(pos + 1) % k], mine[(pos - 1) % k]
+    near = [nxt, prv]
     p = far[pos]
-    fa = far[(pos - 1) % k]
-    fb = far[(pos + 1) % k]
+    fa, fb = far[(pos - 1) % k], far[(pos + 1) % k]
     OFF = topo.mask(core, cores[p])
     ON = topo.mask(core, cores[nxt])
 
-    def die_mates(j):
-        return sum(topo.chip(cores[i]) == topo.chip(cores[j]) and topo.die(cores[i]) == topo.die(cores[j]) for i in range(N))
+    def cut(j, t, h):
+        lo = 2 * NC * j + NC * t
+        return slice(lo, lo + NC) if h is None else slice(lo + HC * h, lo + HC * h + HC)
 
-    def xcols(j):
-        return slice(2 * NC * j, 2 * NC * j + NC)
+    def wait(q, sem, n):
+        q.wait_ge(S[sem], n)
 
-    def tcols(j):
-        return slice(2 * NC * j + NC, 2 * NC * j + 2 * NC)
-
-    def both(j):
-        return slice(2 * NC * j, 2 * NC * j + 2 * NC)
-
-    sync.dma_start(T.xin[:], T.x[:]).then_inc(S["lx"], 16)
-    half = 2 * SW * G
-    for h in (0, 1):
-        sync.dma_start(T.ain[:, h * half:(h + 1) * half], T.a[:, h * half:(h + 1) * half]).then_inc(S["la%d" % h], 16)
+    xw, aw = 4 * HC, 2 * SW * G
+    for h in HALVES:
+        sync.dma_start(T.xin[:, xw * h:xw * h + xw], T.x[:, xw * h:xw * h + xw]).then_inc(S["lx%d" % h], 16)
+    for h in HALVES:
+        sync.dma_start(T.ain[:, aw * h:aw * h + aw], T.a[:, aw * h:aw * h + aw]).then_inc(S["la%d" % h], 16)
     sync.dma_start(T.win[:], T.w[:]).then_inc(S["lw"], 16)
     sync.dma_start(T.bin[:], T.bb[:]).then_inc(S["lb"], 16)
 
     out = []
 
-    def send(cols, dsts, mask, sem):
+    def send(what, cols, dsts, mask, sem):
         ids = []
         for d in dsts:
             rid, pid = topo.addr(cores[d])[:2]
             ids.append(DstId(rid=rid, pnc=pid))
-        for view in (T.qc[:, cols].bitcast(dt.uint8), T.qs[:, cols]):
-            g.remote_dma_fused([RemoteDMATransfer(dst_ids=ids, dma_engine_mask=mask, remote_sem=S[sem],
-                                                  srcs=[view], dsts=[view] * len(ids))], local_sem=S["sent"])
-            out.append(ones(mask))
+        view = T.qs[:, cols] if what == "scales" else T.qc[:, cols].bitcast(dt.uint8)
+        g.remote_dma_fused([RemoteDMATransfer(dst_ids=ids, dma_engine_mask=mask, remote_sem=S[sem],
+                                              srcs=[view], dsts=[view] * len(ids))], local_sem=S["sent"])
+        out.append(ones(mask))
 
-    g.wait_ge(S["qx"], 1)
-    send(xcols(r), [p], OFF, "ax%d" % r)
-    g.wait_ge(S["tq%d" % r], 1)
-    send(both(r), [nxt, prv], ON, "at%d" % r)
-    g.wait_ge(S["ax%d" % p], 2 * ones(OFF))
-    send(xcols(p), [nxt, prv], ON, "ax%d" % p)
-    g.wait_ge(S["tq%d" % p], 1)
-    send(tcols(p), [prv], ON, "at%d" % p)
-    g.wait_ge(S["sent"], sum(out))
+    def send_both(cols, dsts, mask, sem):
+        send("codes", cols, dsts, mask, sem)
+        send("scales", cols, dsts, mask, sem)
 
-    x_here = {r: ("qx", 1), p: ("ax%d" % p, 2 * ones(OFF))}
-    t_here = {j: ("tq%d" % j, 1) for j in (r, p, fa)}
-    for j in (nxt, prv):
-        x_here[j] = t_here[j] = ("at%d" % j, 2 * ones(ON))
-    for j in (fa, fb):
-        x_here[j] = ("ax%d" % j, 2 * ones(ON))
-    t_here[fb] = ("at%d" % fb, 2 * ones(ON))
+    wait(g, "qx0", 1)
+    send("codes", cut(r, 0, 0), [p], OFF, "ah%d" % r)
+    wait(g, "qx1", 1)
+    send("scales", cut(r, 0, None), [p], OFF, "ah%d" % r)
+    send("codes", cut(r, 0, 1), [p], OFF, "ax%d" % r)
+    send_both(cut(r, 0, None), near, ON, "ax%d" % r)
+    for h in HALVES:
+        wait(g, "tq0_%d" % h, 1)
+    send_both(cut(r, 1, None), near, ON, "at%d" % r)
+    wait(g, "ah%d" % p, 2 * ones(OFF))
+    wait(g, "ax%d" % p, ones(OFF))
+    send_both(cut(p, 0, None), near, ON, "ax%d" % p)
+    for h in HALVES:
+        wait(g, "tq1_%d" % h, 1)
+    send_both(cut(p, 1, None), near, ON, "at%d" % p)
+    wait(g, "sent", sum(out))
 
-    seq = [("t", r), ("w", r), ("b", r), ("t", p), ("w", nxt), ("w", prv), ("b", nxt), ("b", prv), ("w", p), ("b", p)]
-    if die_mates(fb) < die_mates(fa):
-        seq += [("t", fa), ("w", fb), ("b", fb), ("w", fa), ("b", fa)]
-    else:
-        seq += [("t", fa), ("w", fa), ("w", fb), ("b", fa), ("b", fb)]
-    order = [j for kind, j in seq if kind == "b"]
-    ybank, before = {}, {}
-    opened = [j for kind, j in seq if kind == "w"]
-    for i, j in enumerate(opened):
-        ybank[j] = G + i % (8 - G)
-        before[j] = opened[i - (8 - G)] if i >= 8 - G else None
+    x_half = {r: [[("qx0", 1)], [("qx1", 1)]],
+              p: [[("ah%d" % p, 2 * ones(OFF))], [("ax%d" % p, ones(OFF))]]}
+    x_here = {j: x_half[j][0] + x_half[j][1] for j in (r, p)}
+    t_here = {j: [("tq%d_%d" % (u, h), 1) for h in HALVES] for u, j in ((0, r), (1, p))}
+    for j in near + [fa, fb]:
+        x_here[j] = [("ax%d" % j, 2 * ones(ON))]
+        t_here[j] = [("at%d" % j, 2 * ones(ON))]
 
-    def bank(i):
-        return T.ps[:, 512 * i:512 * i + NC]
+    def waits(q, pairs):
+        for sem, n in pairs:
+            wait(q, sem, n)
 
-    vec.wait_ge(S["lx"], 16)
-    vec.quantize_mx(T.qc[:, xcols(r)], T.qs[:, xcols(r)], T.xin[:]).then_inc(S["qx"], 1)
-    for h in (0, 1):
+    def bank(i, n):
+        return T.ps[:, 512 * i:512 * i + n]
+
+    for h in HALVES:
+        wait(vec, "lx%d" % h, 16)
+        vec.quantize_mx(T.qc[:, cut(r, 0, h)], T.qs[:, cut(r, 0, h)], T.xin[:, xw * h:xw * h + xw]).then_inc(S["qx%d" % h], 1)
+    for h in HALVES:
         c = slice(2 * SW * h, 2 * SW * h + 2 * SW)
-        vec.wait_ge(S["la%d" % h], 16)
-        vec.quantize_mx(T.ac[:, c], T.asc[:, c], T.ain[:, h * half:(h + 1) * half]).then_inc(S["qa%d" % h], 1)
+        wait(vec, "la%d" % h, 16)
+        vec.quantize_mx(T.ac[:, c], T.asc[:, c], T.ain[:, aw * h:aw * h + aw]).then_inc(S["qa%d" % h], 1)
 
-    last_t = None
-    for kind, j in seq:
-        X = (T.qc[:, xcols(j)], T.qs[:, xcols(j)])
-        tt = (T.qc[:, tcols(j)], T.qs[:, tcols(j)])
-        if kind == "t":
-            ten.wait_ge(S[x_here[j][0]], x_here[j][1])
+    used = []
+
+    def make_t(j, u):
+        tile = T["t%d" % u]
+        for h in HALVES:
+            waits(ten, x_half[j][h])
             for b in range(G):
-                if last_t is None:
-                    ten.wait_ge(S["qa%d" % (b // 2)], 1)
+                if not used:
+                    wait(ten, "qa%d" % (b // 2), 1)
                 else:
-                    ten.wait_ge(S["sc%d_%d" % (last_t, b)], 1)
+                    wait(ten, "sc%d_%d_%d" % (used[-1] + (b,)), 1)
                 c = slice(SW * b, SW * b + SW)
-                ten.matmul_mx(bank(b), T.ac[:, c], T.asc[:, c], X[0], X[1], True, True).then_inc(S["mt%d_%d" % (j, b)], 1)
-                cols = T["tb%d" % j][:, b:G * NC:G]
+                ten.matmul_mx(bank(b, HC), T.ac[:, c], T.asc[:, c], T.qc[:, cut(j, 0, h)], T.qs[:, cut(j, 0, h)],
+                              True, True).then_inc(S["mt%d_%d_%d" % (u, h, b)], 1)
+                cols = tile[:, xw * h + b:xw * h + xw:G]
+                done = S["sc%d_%d_%d" % (u, h, b)]
                 if b % 2 == 0:
-                    act.wait_ge(S["mt%d_%d" % (j, b)], 1)
-                    act.activation(cols, bank(b), ActivationFunctionType.Copy, scale=FACTOR).then_inc(S["sc%d_%d" % (j, b)], 1)
+                    wait(act, "mt%d_%d_%d" % (u, h, b), 1)
+                    act.activation(cols, bank(b, HC), ActivationFunctionType.Copy, scale=FACTOR).then_inc(done, 1)
                 else:
-                    vec.wait_ge(S["mt%d_%d" % (j, b)], 1)
-                    vec.tensor_scalar(cols, bank(b), FACTOR, None, AluOpType.mult).then_inc(S["sc%d_%d" % (j, b)], 1)
+                    wait(vec, "mt%d_%d_%d" % (u, h, b), 1)
+                    vec.tensor_scalar(cols, bank(b, HC), FACTOR, None, AluOpType.mult).then_inc(done, 1)
             for b in range(G):
-                vec.wait_ge(S["sc%d_%d" % (j, b)], 1)
-            vec.quantize_mx(tt[0], tt[1], T["tb%d" % j][:]).then_inc(S["tq%d" % j], 1)
-            if last_t is None:
-                vec.wait_ge(S["lw"], 16)
-                vec.quantize_mx(T.wc[:], T.wsc[:], T.win[:]).then_inc(S["qw"], 1)
-                vec.wait_ge(S["lb"], 16)
-                vec.quantize_mx(T.bc[:], T.bsc[:], T.bin[:]).then_inc(S["qb"], 1)
-            last_t = j
-        elif kind == "w":
-            ten.wait_ge(S["qw"], 1)
-            ten.wait_ge(S[x_here[j][0]], x_here[j][1])
-            if before[j] is not None:
-                ten.wait_ge(S["ev%d" % before[j]], 1)
-            ten.matmul_mx(bank(ybank[j]), T.wc[:], T.wsc[:], X[0], X[1], True, False)
-        else:
-            ten.wait_ge(S["qb"], 1)
-            ten.wait_ge(S[t_here[j][0]], t_here[j][1])
-            ten.matmul_mx(bank(ybank[j]), T.bc[:], T.bsc[:], tt[0], tt[1], False, True).then_inc(S["yd%d" % j], 1)
-            dst = T.yo[:, NC * j:NC * j + NC]
-            q = act if order.index(j) % 2 == 0 else vec
-            q.wait_ge(S["yd%d" % j], 1)
-            if q is act:
-                act.activation(dst, bank(ybank[j]), ActivationFunctionType.Copy).then_inc(S["ev%d" % j], 1)
-            else:
-                vec.tensor_copy(dst, bank(ybank[j])).then_inc(S["ev%d" % j], 1)
+                wait(vec, "sc%d_%d_%d" % (u, h, b), 1)
+            vec.quantize_mx(T.qc[:, cut(j, 1, h)], T.qs[:, cut(j, 1, h)],
+                            tile[:, xw * h:xw * h + xw]).then_inc(S["tq%d_%d" % (u, h)], 1)
+            used.append((u, h))
 
-    groups = [mine] + [[j] for j in order if j in far]
+    def term_w(j, i, h=None):
+        n = NC if h is None else HC
+        ten.matmul_mx(bank(i, n), T.wc[:], T.wsc[:], T.qc[:, cut(j, 0, h)], T.qs[:, cut(j, 0, h)], True, False)
+
+    def term_b(j, i, q, h=None):
+        n, s = (NC, 0) if h is None else (HC, h)
+        ten.matmul_mx(bank(i, n), T.bc[:], T.bsc[:], T.qc[:, cut(j, 1, h)], T.qs[:, cut(j, 1, h)],
+                      False, True).then_inc(S["yd%d_%d" % (j, s)], 1)
+        wait(q, "yd%d_%d" % (j, s), 1)
+        dst = T.yo[:, NC * j + HC * s:NC * j + HC * s + n]
+        if q is act:
+            act.activation(dst, bank(i, n), ActivationFunctionType.Copy).then_inc(S["ev%d_%d" % (j, s)], 1)
+        else:
+            vec.tensor_copy(dst, bank(i, n)).then_inc(S["ev%d_%d" % (j, s)], 1)
+
+    make_t(r, 0)
+    wait(vec, "lw", 16)
+    vec.quantize_mx(T.wc[:], T.wsc[:], T.win[:]).then_inc(S["qw"], 1)
+    wait(vec, "lb", 16)
+    vec.quantize_mx(T.bc[:], T.bsc[:], T.bin[:]).then_inc(S["qb"], 1)
+    wait(ten, "qw", 1)
+    term_w(r, G)
+    wait(ten, "qb", 1)
+    waits(ten, t_here[r])
+    term_b(r, G, act)
+    make_t(p, 1)
+    for i, j in enumerate(near):
+        waits(ten, x_here[j])
+        term_w(j, G + 1 + i)
+    for i, j in enumerate(near):
+        waits(ten, t_here[j])
+        term_b(j, G + 1 + i, (vec, act)[i])
+    term_w(p, G + 3)
+    waits(ten, t_here[p])
+    term_b(p, G + 3, vec)
+    for b in range(G):
+        wait(ten, "sc%d_%d_%d" % (used[-1] + (b,)), 1)
+    for i, j in enumerate((fa, fb)):
+        waits(ten, x_here[j])
+        for h in HALVES:
+            term_w(j, 2 * i + h, h)
+    for i, j in enumerate((fa, fb)):
+        waits(ten, t_here[j])
+        for h in HALVES:
+            term_b(j, 2 * i + h, (act, vec)[h], h)
+
+    groups = [mine, [p], [fa], [fb]]
     for js in groups:
         for j in js:
-            sync.wait_ge(S["ev%d" % j], 1)
+            for h in HALVES if j in (fa, fb) else (0,):
+                wait(sync, "ev%d_%d" % (j, h), 1)
         c = slice(NC * js[0], NC * js[-1] + NC)
         sync.dma_start(T.y[:, c], T.yo[:, c]).then_inc(S["st"], 16)
-    sync.wait_ge(S["st"], 16 * len(groups))
+    wait(sync, "st", 16 * len(groups))

import numpy as np
from concourse.bass import DstId, RemoteDMATransfer
from concourse.mybir import dt, AluOpType, ActivationFunctionType

N, NC, G = 6, 256, 4
HC = NC // 2
SW = 128
FACTOR = float(np.float32(0.047))
HALVES = (0, 1)

SCRATCH = {
    "xin": ("sbuf", [128, 4 * NC], "bfloat16"),
    "ain": ("sbuf", [128, 4 * SW * G], "bfloat16"),
    "win": ("sbuf", [128, 4 * SW], "bfloat16"),
    "bin": ("sbuf", [128, 4 * SW], "bfloat16"),
    "t0": ("sbuf", [128, 4 * NC], "bfloat16"),
    "t1": ("sbuf", [128, 4 * NC], "bfloat16"),
    "ac": ("sbuf", [128, SW * G], "float8_e4m3fn_x4"),
    "asc": ("sbuf", [128, SW * G], "uint8"),
    "wc": ("sbuf", [128, SW], "float8_e4m3fn_x4"),
    "wsc": ("sbuf", [128, SW], "uint8"),
    "bc": ("sbuf", [128, SW], "float8_e4m3fn_x4"),
    "bsc": ("sbuf", [128, SW], "uint8"),
    "qc": ("sbuf", [128, 2 * NC * N], "float8_e4m3fn_x4"),
    "qs": ("sbuf", [128, 2 * NC * N], "uint8"),
    "yo": ("sbuf", [128, N * NC], "float32"),
    "ps": ("psum", [128, 512 * 8], "float32"),
}
SEMAPHORES = ["lx0", "lx1", "la0", "la1", "lw", "lb", "qx0", "qx1", "qa0", "qa1", "qw", "qb", "sent", "st"]
for _j in range(N):
    SEMAPHORES += ["%s%d" % (s, _j) for s in ("ah", "ax", "at")]
    SEMAPHORES += ["%s%d_%d" % (s, _j, h) for s in ("yd", "ev") for h in HALVES]
for _u in (0, 1):
    SEMAPHORES += ["tq%d_%d" % (_u, h) for h in HALVES]
    SEMAPHORES += ["%s%d_%d_%d" % (s, _u, h, b) for s in ("mt", "sc") for h in HALVES for b in range(G)]


def ones(mask):
    return bin(mask).count("1")


def rank_program(g, core, T, topo):
    r = T.rank_of(core)
    if r is None:
        return
    S, cores = T.sem, T.cores
    ten, vec, act, sync = g.tensor, g.vector, g.scalar, g.sync

    mine = [j for j in range(N) if topo.chip(cores[j]) == topo.chip(core)]
    far = [j for j in range(N) if j not in mine]
    k = len(mine)
    pos = mine.index(r)
    nxt, prv = mine[(pos + 1) % k], mine[(pos - 1) % k]
    near = [nxt, prv]
    p = far[pos]
    fa, fb = far[(pos - 1) % k], far[(pos + 1) % k]
    OFF = topo.mask(core, cores[p])
    ON = topo.mask(core, cores[nxt])

    def cut(j, t, h):
        lo = 2 * NC * j + NC * t
        return slice(lo, lo + NC) if h is None else slice(lo + HC * h, lo + HC * h + HC)

    def wait(q, sem, n):
        q.wait_ge(S[sem], n)

    xw, aw = 4 * HC, 2 * SW * G
    for h in HALVES:
        sync.dma_start(T.xin[:, xw * h:xw * h + xw], T.x[:, xw * h:xw * h + xw]).then_inc(S["lx%d" % h], 16)
    for h in HALVES:
        sync.dma_start(T.ain[:, aw * h:aw * h + aw], T.a[:, aw * h:aw * h + aw]).then_inc(S["la%d" % h], 16)
    sync.dma_start(T.win[:], T.w[:]).then_inc(S["lw"], 16)
    sync.dma_start(T.bin[:], T.bb[:]).then_inc(S["lb"], 16)

    out = []

    def send(what, cols, dsts, mask, sem):
        ids = []
        for d in dsts:
            rid, pid = topo.addr(cores[d])[:2]
            ids.append(DstId(rid=rid, pnc=pid))
        view = T.qs[:, cols] if what == "scales" else T.qc[:, cols].bitcast(dt.uint8)
        g.remote_dma_fused([RemoteDMATransfer(dst_ids=ids, dma_engine_mask=mask, remote_sem=S[sem],
                                              srcs=[view], dsts=[view] * len(ids))], local_sem=S["sent"])
        out.append(ones(mask))

    def send_both(cols, dsts, mask, sem):
        send("codes", cols, dsts, mask, sem)
        send("scales", cols, dsts, mask, sem)

    wait(g, "qx0", 1)
    send("codes", cut(r, 0, 0), [p], OFF, "ah%d" % r)
    wait(g, "qx1", 1)
    send("scales", cut(r, 0, None), [p], OFF, "ah%d" % r)
    send("codes", cut(r, 0, 1), [p], OFF, "ax%d" % r)
    send_both(cut(r, 0, None), near, ON, "ax%d" % r)
    for h in HALVES:
        wait(g, "tq0_%d" % h, 1)
    send_both(cut(r, 1, None), near, ON, "at%d" % r)
    wait(g, "ah%d" % p, 2 * ones(OFF))
    wait(g, "ax%d" % p, ones(OFF))
    send_both(cut(p, 0, None), near, ON, "ax%d" % p)
    for h in HALVES:
        wait(g, "tq1_%d" % h, 1)
    send_both(cut(p, 1, None), near, ON, "at%d" % p)
    wait(g, "sent", sum(out))

    x_half = {r: [[("qx0", 1)], [("qx1", 1)]],
              p: [[("ah%d" % p, 2 * ones(OFF))], [("ax%d" % p, ones(OFF))]]}
    x_here = {j: x_half[j][0] + x_half[j][1] for j in (r, p)}
    t_here = {j: [("tq%d_%d" % (u, h), 1) for h in HALVES] for u, j in ((0, r), (1, p))}
    for j in near + [fa, fb]:
        x_here[j] = [("ax%d" % j, 2 * ones(ON))]
        t_here[j] = [("at%d" % j, 2 * ones(ON))]

    def waits(q, pairs):
        for sem, n in pairs:
            wait(q, sem, n)

    def bank(i, n):
        return T.ps[:, 512 * i:512 * i + n]

    for h in HALVES:
        wait(vec, "lx%d" % h, 16)
        vec.quantize_mx(T.qc[:, cut(r, 0, h)], T.qs[:, cut(r, 0, h)], T.xin[:, xw * h:xw * h + xw]).then_inc(S["qx%d" % h], 1)
    for h in HALVES:
        c = slice(2 * SW * h, 2 * SW * h + 2 * SW)
        wait(vec, "la%d" % h, 16)
        vec.quantize_mx(T.ac[:, c], T.asc[:, c], T.ain[:, aw * h:aw * h + aw]).then_inc(S["qa%d" % h], 1)

    used = []

    def make_t(j, u):
        tile = T["t%d" % u]
        for h in HALVES:
            waits(ten, x_half[j][h])
            for b in range(G):
                if not used:
                    wait(ten, "qa%d" % (b // 2), 1)
                else:
                    wait(ten, "sc%d_%d_%d" % (used[-1] + (b,)), 1)
                c = slice(SW * b, SW * b + SW)
                ten.matmul_mx(bank(b, HC), T.ac[:, c], T.asc[:, c], T.qc[:, cut(j, 0, h)], T.qs[:, cut(j, 0, h)],
                              True, True).then_inc(S["mt%d_%d_%d" % (u, h, b)], 1)
                cols = tile[:, xw * h + b:xw * h + xw:G]
                done = S["sc%d_%d_%d" % (u, h, b)]
                if b % 2 == 0:
                    wait(act, "mt%d_%d_%d" % (u, h, b), 1)
                    act.activation(cols, bank(b, HC), ActivationFunctionType.Copy, scale=FACTOR).then_inc(done, 1)
                else:
                    wait(vec, "mt%d_%d_%d" % (u, h, b), 1)
                    vec.tensor_scalar(cols, bank(b, HC), FACTOR, None, AluOpType.mult).then_inc(done, 1)
            for b in range(G):
                wait(vec, "sc%d_%d_%d" % (u, h, b), 1)
            vec.quantize_mx(T.qc[:, cut(j, 1, h)], T.qs[:, cut(j, 1, h)],
                            tile[:, xw * h:xw * h + xw]).then_inc(S["tq%d_%d" % (u, h)], 1)
            used.append((u, h))

    def term_w(j, i, h=None):
        n = NC if h is None else HC
        ten.matmul_mx(bank(i, n), T.wc[:], T.wsc[:], T.qc[:, cut(j, 0, h)], T.qs[:, cut(j, 0, h)], True, False)

    def term_b(j, i, q, h=None):
        n, s = (NC, 0) if h is None else (HC, h)
        ten.matmul_mx(bank(i, n), T.bc[:], T.bsc[:], T.qc[:, cut(j, 1, h)], T.qs[:, cut(j, 1, h)],
                      False, True).then_inc(S["yd%d_%d" % (j, s)], 1)
        wait(q, "yd%d_%d" % (j, s), 1)
        dst = T.yo[:, NC * j + HC * s:NC * j + HC * s + n]
        if q is act:
            act.activation(dst, bank(i, n), ActivationFunctionType.Copy).then_inc(S["ev%d_%d" % (j, s)], 1)
        else:
            vec.tensor_copy(dst, bank(i, n)).then_inc(S["ev%d_%d" % (j, s)], 1)

    make_t(r, 0)
    wait(vec, "lw", 16)
    vec.quantize_mx(T.wc[:], T.wsc[:], T.win[:]).then_inc(S["qw"], 1)
    wait(vec, "lb", 16)
    vec.quantize_mx(T.bc[:], T.bsc[:], T.bin[:]).then_inc(S["qb"], 1)
    wait(ten, "qw", 1)
    term_w(r, G)
    wait(ten, "qb", 1)
    waits(ten, t_here[r])
    term_b(r, G, act)
    make_t(p, 1)
    for i, j in enumerate(near):
        waits(ten, x_here[j])
        term_w(j, G + 1 + i)
    for i, j in enumerate(near):
        waits(ten, t_here[j])
        term_b(j, G + 1 + i, (vec, act)[i])
    term_w(p, G + 3)
    waits(ten, t_here[p])
    term_b(p, G + 3, vec)
    for b in range(G):
        wait(ten, "sc%d_%d_%d" % (used[-1] + (b,)), 1)
    for i, j in enumerate((fa, fb)):
        waits(ten, x_here[j])
        for h in HALVES:
            term_w(j, 2 * i + h, h)
    for i, j in enumerate((fa, fb)):
        waits(ten, t_here[j])
        for h in HALVES:
            term_b(j, 2 * i + h, (act, vec)[h], h)

    groups = [mine, [p], [fa], [fb]]
    for js in groups:
        for j in js:
            for h in HALVES if j in (fa, fb) else (0,):
                wait(sync, "ev%d_%d" % (j, h), 1)
        c = slice(NC * js[0], NC * js[-1] + NC)
        sync.dma_start(T.y[:, c], T.yo[:, c]).then_inc(S["st"], 16)
    wait(sync, "st", 16 * len(groups))
